import numpy as np
import ml_dtypes


def mxq(x, axis, fmt="e4m3"):
    dtype, down = {"e4m3": (ml_dtypes.float8_e4m3fn, 7), "e5m2": (ml_dtypes.float8_e5m2, 14)}[fmt]
    v = np.moveaxis(np.asarray(x, np.float32).astype(ml_dtypes.bfloat16).astype(np.float64), axis, -1)
    blocks = v.reshape(v.shape[:-1] + (-1, 32))
    amax = np.abs(blocks).max(-1, keepdims=True)
    byte = np.maximum(np.where(amax > 0, np.frexp(amax)[1] - 1 + 127, 0) - down, 1)
    scale = np.exp2(byte - 127.0)
    codes = (blocks / scale).astype(np.float32).astype(dtype).astype(np.float64)
    return np.moveaxis((codes * scale).reshape(v.shape), -1, axis)


WIDE = False


def mx_kscale(k):
    if not WIDE:
        return np.ones(k)
    levels = np.array([10, -10, 5, -5, 0])
    if k % 512:
        return np.exp2(np.random.permutation(np.resize(levels, k // 32))).repeat(32)
    a = np.empty((k // 512, 16))
    for p in range(k // 512):
        a[p, :8] = np.random.permutation(np.resize(levels, 8))
        for g in range(8):
            far = levels[np.abs(levels - a[p, g]) >= 10]
            a[p, g + 8] = far[np.random.randint(len(far))]
    return np.exp2(a.ravel()).repeat(32)


def f64(x):
    return np.asarray(x).astype(np.float64)


def striped(idx):
    return np.tile(idx.reshape(-1, 16).T, (8, 1)).astype(np.uint16)


def unstriped(offs):
    return offs[:16].T.reshape(-1).astype(np.int64)


E2M1 = np.array([0.0, 0.5, 1.0, 1.5, 2.0, 3.0, 4.0, 6.0, -0.0, -0.5, -1.0, -1.5, -2.0, -3.0, -4.0, -6.0])


def pack_weight(w, fmt):
    k, n = w.shape
    w = f64(np.asarray(w, np.float32).astype(ml_dtypes.bfloat16)).reshape(k // 32, 32, n)
    amax = np.abs(w).max(1)
    if fmt == "e4m3":
        byte = np.frexp(amax)[1] - 1 + 127 - 7
    else:
        mant, ex = np.frexp(amax / 6.0)
        byte = np.where(mant > 0.5, ex, ex - 1) + 127
    byte = np.clip(np.where(amax > 0, byte, 1), 1, 254)
    scaled = (w * np.exp2(127.0 - byte)[:, None, :]).reshape(k, n).astype(np.float32)
    by_word = np.ascontiguousarray(scaled.reshape(k // 512, 128, 4, n).transpose(0, 1, 3, 2))
    if fmt == "e4m3":
        words = by_word.astype(ml_dtypes.float8_e4m3fn).view(np.uint8)
    else:
        c = by_word.astype(ml_dtypes.float4_e2m1fn).view(np.uint8) & 0xF
        words = (c[..., 0::2] | (c[..., 1::2] << 4)).reshape(k // 512, 128, 2 * n)
    return np.ascontiguousarray(words), np.ascontiguousarray(byte.astype(np.uint8).reshape(k // 512, 16, n))


def unpack_weight(words, scales, fmt):
    g, _, n = scales.shape
    words = np.ascontiguousarray(words).reshape(g, 128, n, -1)
    if fmt == "e4m3":
        vals = words.view(ml_dtypes.float8_e4m3fn).astype(np.float64)
    else:
        nib = np.empty((g, 128, n, 4), np.uint8)
        nib[..., 0::2] = words & 0xF
        nib[..., 1::2] = words >> 4
        vals = E2M1[nib]
    vals = vals * np.repeat(np.exp2(scales.astype(np.float64) - 127.0), 8, axis=1)[..., None]
    return vals.transpose(0, 1, 3, 2).reshape(g * 512, n)


def gelu(v):
    return 0.5 * v * (1.0 + np.tanh(np.sqrt(2.0 / np.pi) * (v + 0.044715 * v**3)))


K, T, S, P, H, N = 1536, 2048, 1024, 512, 1024, 512

def setup_inputs():
    n = np.random.standard_normal
    s = mx_kscale(K)[:, None]
    u = mx_kscale(H)[:, None]
    tab_words, tab_scales = pack_weight(n((K, T)) * s, "e4m3")
    w2_words, w2_scales = pack_weight(n((H, N)) / np.sqrt(H) / u, "e2m1")
    perm = np.random.permutation(S)
    return {
        "tab_words": tab_words, "tab_scales": tab_scales,
        "offs": striped(np.random.permutation(T)[:S]),
        "pos1": striped(perm[:P]),
        "pos2": striped(perm[P:]),
        "w1": (0.55 * n((K, H)) / np.sqrt(K) / s).astype(np.float32),
        "base": (0.5 * n((H, S))).astype(np.float32),
        "temp": np.random.uniform(0.4, 1.6, H).astype(np.float32),
        "shift": (0.5 * n(H)).astype(np.float32),
        "sgn": (0.4 * n(H)).astype(np.float32),
        "low": (0.4 * n(H) - 0.2).astype(np.float32),
        "wgs": np.exp(0.3 * n((128, P))).astype(np.float32),
        "gain": (np.random.uniform(0.6, 1.6, H) * u[:, 0]).astype(np.float32),
        "w2_words": w2_words, "w2_scales": w2_scales,
        "w3": (n((H, N)) / np.sqrt(H) / u).astype(np.float32),
    }

def reference(tab_words, tab_scales, offs, pos1, pos2, w1, base, temp, shift, sgn, low, wgs, gain, w2_words, w2_scales, w3):
    v = unpack_weight(tab_words, tab_scales, "e4m3")[:, unstriped(offs)]
    h = (mxq(f64(w1), 0, "e4m3").T @ v) + f64(base)
    look = np.exp(f64(temp)[:, None] * h[:, unstriped(pos1)] + f64(shift)[:, None])
    a = f64(sgn)[:, None] * look
    page = np.maximum(h, f64(low)[:, None])
    page[:, unstriped(pos2)] = np.tile(f64(wgs), (H // 128, 1)) * a
    hq = mxq(f64(gain)[:, None] * page, 0, "e4m3")
    y2 = unpack_weight(w2_words, w2_scales, "e2m1").T @ hq
    y3 = mxq(f64(w3), 0, "e4m3").T @ hq
    return np.maximum(y2, y3)

from contextlib import ExitStack

import concourse.mybir as mybir
from concourse.masks import make_identity

K, T, S, PICK, H, N = 1536, 2048, 1024, 512, 1024, 512
FLOPS = 2 * K * H * S + 2 * 2 * H * N * S

F32 = mybir.dt.float32
BF16 = mybir.dt.bfloat16
I32 = mybir.dt.int32
U32 = mybir.dt.uint32
U16 = mybir.dt.uint16
U8 = mybir.dt.uint8
FP8X4 = mybir.dt.float8_e4m3fn_x4
FP4X4 = mybir.dt.float4_e2m1fn_x4
ACT = mybir.ActivationFunctionType
ALU = mybir.AluOpType

P = 128
PACK = 4
PASS = P * PACK
BANK = 512
K_PASSES = K // PASS
R_PASSES = H // PASS
ROW_TILES = H // P
HALVES = S // BANK
N_TILES = N // P


def tile_list_dead_pixel_readout_kernel(
    tc, tab_words, tab_scales, offs, pos1, pos2, w1, base, temp, shift, sgn, low, wgs, gain,
    w2_words, w2_scales, w3, out,
):
    nc = tc.nc
    with ExitStack() as ctx:
        lists = ctx.enter_context(tc.tile_pool(name="lists", bufs=1))
        keep = ctx.enter_context(tc.tile_pool(name="keep", bufs=1))
        stage = ctx.enter_context(tc.tile_pool(name="stage", bufs=4))
        ring = ctx.enter_context(tc.tile_pool(name="ring", bufs=3))
        psum = ctx.enter_context(tc.psum_pool(name="psum", bufs=1))

        def bank(index):
            return psum.tile([P, BANK], F32, name="bank", tag="bank%d" % index)

        def kept(name, shape, dtype):
            return keep.tile(shape, dtype, name=name, tag=name, align_bytes=64)

        offs_t = lists.tile([P, S // 16], U16, name="offs_t")
        pos1_t = lists.tile([P, PICK // 16], U16, name="pos1_t")
        pos2_t = lists.tile([P, PICK // 16], U16, name="pos2_t")
        table_scales = kept("table_scales", [P, T], U8)
        nc.gpsimd.memset(table_scales[:].bitcast(I32), 0)
        identity = kept("identity", [P, P], F32)
        make_identity(nc, identity[:])

        per_row = {}

        def load_per_row(queue, name, values):
            per_row[name] = kept(name + "_t", [P, ROW_TILES], F32)
            queue.dma_start(
                out=per_row[name][:].rearrange("p (b t) -> p b t", t=PACK),
                in_=values.rearrange("(b p t) -> p b t", p=P, t=PACK),
            )

        def column(name, tile_index):
            return per_row[name][:, tile_index : tile_index + 1]

        table_words = []

        def load_table_words(a):
            words = kept("table_words%d" % a, [P, T], U32)
            nc.sync.dma_start(
                out=words[:].bitcast(I32), in_=tab_words[a].rearrange("p c i -> p (c i)").bitcast(I32)
            )
            table_words.append(words)

        wgs_rows = kept("wgs_rows", [P, PICK], F32)
        nc.sync.dma_start(out=wgs_rows[:], in_=wgs)
        load_per_row(nc.scalar, "sgn", sgn)
        load_table_words(0)
        nc.sync.dma_start(offs_t[:], offs)
        def load_rows(weight, a, cols, tag):
            width = cols.stop - cols.start
            raw = stage.tile([P, PACK, width], F32, name="raw", tag=tag, bufs=4 if tag == "raw" else 2)
            nc.sync.dma_start(
                out=raw[:], in_=weight[a * PASS : (a + 1) * PASS, cols].rearrange("(p j) c -> p j c", j=PACK)
            )
            return raw

        base_rows = base.rearrange("(b p t) j -> b t p j", p=P, t=PACK)
        h_tiles = []

        def load_base(i):
            h = kept("h%d" % i, [P, S], F32)
            nc.sync.dma_start(out=h[:], in_=base_rows[i // PACK, i % PACK])
            h_tiles.append(h)

        w1_raw = {}
        w1_raw[0, 0] = load_rows(w1, 0, slice(0, PASS), "raw")
        for quad in range(4):
            nc.sync.dma_start(
                out=table_scales[32 * quad : 32 * quad + 4 * K_PASSES, :].bitcast(I32),
                in_=tab_scales[:, 4 * quad : 4 * quad + 4, :].bitcast(I32),
            )
        w1_raw[0, 1] = load_rows(w1, 1, slice(0, PASS), "raw")
        load_table_words(1)
        load_table_words(2)
        w1_last = [load_rows(w1, 2, slice(c * 256, (c + 1) * 256), "raw_half") for c in range(2)]
        load_base(0)
        nc.sync.dma_start(pos1_t[:], pos1)
        load_per_row(nc.sync, "low", low)
        load_per_row(nc.sync, "temp", temp)
        load_per_row(nc.sync, "shift", shift)
        nc.sync.dma_start(pos2_t[:], pos2)
        load_base(1)
        load_per_row(nc.sync, "gain", gain)

        turned = bank(3)
        for mb in range(PICK // P):
            cols = slice(mb * P, (mb + 1) * P)
            nc.tensor.transpose(turned[:, cols], wgs_rows[:, cols], identity[:])
        dealt = kept("rounded0", [P, PICK // P, PACK, P], F32)
        for rep in range(4):
            nc.scalar.copy(
                out=dealt[:, :, :, 32 * rep : 32 * (rep + 1)],
                in_=turned[:].rearrange("m (b q t) -> m b t q", q=32, t=PACK),
            )

        picked_scales = kept("picked_scales", [P, S], U8)
        picked_words = []
        for a in range(K_PASSES):
            if a == 1:
                nc.vector.tensor_copy(picked_scales[:], table_scales[:].indirect(offs_t[:]))
            words = kept("picked_words%d" % a, [P, S], U32)
            nc.vector.tensor_copy(words[:], table_words[a][:].indirect(offs_t[:]))
            picked_words.append(words)

        def grouped_tile():
            return ring.tile([P, PACK * BANK], BF16, name="grouped", tag="grouped", align_bytes=64)

        def copy_on(engine, dst, src):
            if engine == "vector":
                nc.vector.tensor_copy(out=dst, in_=src)
            else:
                nc.scalar.copy(out=dst, in_=src)

        def group_w1(engine, grouped, raw, first, count):
            dst = grouped[:].rearrange("p (t m j) -> p m j t", t=PACK, j=PACK)[:, first : first + count]
            copy_on(engine, dst, raw.rearrange("p j (m t) -> p m j t", t=PACK))

        def group_plain(engine, grouped, planes, first, count):
            dst = grouped[:, PACK * first : PACK * (first + count)].rearrange("p (c i j) -> p c j i", i=4, j=PACK)
            copy_on(engine, dst, planes.rearrange("p j (c i) -> p c j i", i=4))

        def quantise(name, grouped, pieces, codes_slot=None):
            codes = kept(codes_slot or name + "_codes", [P, BANK], U32)
            scales = kept(name + "_scales", [P, BANK], U8)
            width = BANK // pieces
            for c in range(pieces):
                cols = slice(c * width, (c + 1) * width)
                nc.vector.quantize_mx(
                    out=codes[:, cols].bitcast(FP8X4),
                    scales=scales[:, cols],
                    in_=grouped[:, PACK * c * width : PACK * (c + 1) * width],
                )
            return codes, scales

        w1_q = {}
        g0 = grouped_tile()
        group_w1("scalar", g0, w1_raw[0, 0][:], 0, P)
        w1_q[0, 0] = quantise("w1_00", g0, 1)
        g1 = grouped_tile()
        group_w1("scalar", g1, w1_raw[0, 1][:], 0, P)
        halves = []
        for c, engine in enumerate(("scalar", "vector")):
            grouped = ring.tile([P, PACK * 256], BF16, name="grouped_half", tag="grouped_half", bufs=3, align_bytes=64)
            copy_on(
                engine,
                grouped[:].rearrange("p (t m j) -> p m j t", t=PACK, j=PACK),
                w1_last[c][:].rearrange("p j (m t) -> p m j t", t=PACK),
            )
            halves.append(grouped)
            if c == 0:
                w1_q[0, 1] = quantise("w1_01", g1, 1)
        codes = kept("w1_02_codes", [P, BANK], U32)
        scales = kept("w1_02_scales", [P, BANK], U8)
        for t in range(PACK):
            for c in range(2):
                cols = slice(t * P + 64 * c, t * P + 64 * (c + 1))
                nc.vector.quantize_mx(
                    out=codes[:, cols].bitcast(FP8X4), scales=scales[:, cols],
                    in_=halves[c][:, 256 * t : 256 * (t + 1)],
                )
        w1_q[0, 2] = (codes, scales)

        signed = kept("signed", [P, ROW_TILES, PICK], F32)
        for t in range(PACK):
            back = bank(4 + t)
            for mb in range(PICK // P):
                nc.tensor.transpose(back[:, mb * P : (mb + 1) * P], dealt[:, mb, t, :], identity[:])
            for b in range(R_PASSES):
                i = PACK * b + t
                nc.scalar.activation(out=signed[:, i, :], in_=back[:], func=ACT.Copy, scale=column("sgn", i))

        w3_raw = {}
        for a in range(K_PASSES):
            w1_raw[1, a] = load_rows(w1, a, slice(PASS, 2 * PASS), "raw")
            load_base(2 + a)
        for b in range(R_PASSES):
            w3_raw[b] = load_rows(w3, b, slice(0, N), "raw")
            load_base(5 + b)
        w2_codes = kept("w2_codes", [P, R_PASSES, 2 * N], U8)
        nc.sync.dma_start(
            out=w2_codes[:].bitcast(I32), in_=w2_words.rearrange("b p c -> p b c").bitcast(I32)
        )
        load_base(7)
        w2_planes = kept("w2_planes", [P, R_PASSES, N], U8)
        nc.gpsimd.memset(w2_planes[:].rearrange("p b c -> p (b c)").bitcast(I32), 0)
        for quad in range(4):
            nc.gpsimd.dma_start(
                out=w2_planes[32 * quad : 32 * quad + 4, :, :].bitcast(I32),
                in_=w2_scales[:, 4 * quad : 4 * quad + 4, :].rearrange("b r c -> r b c").bitcast(I32),
            )

        looks, pages = {}, {}
        rounded = [kept("rounded%d" % b, [P, PACK, S], BF16) for b in range(R_PASSES)]

        h_acc = {}

        def first_pass(i, a):
            b, t = divmod(i, PACK)
            rows = slice(t * P, (t + 1) * P)
            codes, scales = w1_q[b, a]
            for half in range(HALVES):
                cols = slice(half * BANK, (half + 1) * BANK)
                if a == 0:
                    h_acc[i, half] = bank(2 * (i % 2) + half)
                nc.tensor.matmul_mx(
                    out=h_acc[i, half][:],
                    lhsT=codes[:, rows].bitcast(FP8X4),
                    lhsT_scale=scales[:, rows],
                    rhs=picked_words[a][:, cols].bitcast(FP8X4),
                    rhs_scale=picked_scales[4 * a : P, cols],
                    start=(a == 0),
                    stop=(a == K_PASSES - 1),
                )

        def add_base(i):
            for half in range(HALVES):
                cols = slice(half * BANK, (half + 1) * BANK)
                nc.vector.tensor_tensor(
                    out=h_tiles[i][:, cols], in0=h_acc[i, half][:], in1=h_tiles[i][:, cols], op=ALU.add
                )

        def look(i):
            looks[i] = ring.tile([P, PICK], F32, name="look", tag="look")
            nc.scalar.activation(
                out=looks[i][:], in_=h_tiles[i][:].indirect(pos1_t[:]), func=ACT.Exp,
                bias=column("shift", i), scale=column("temp", i),
            )

        def floor(i):
            pages[i] = ring.tile([P, S], F32, name="page", tag="page")
            nc.vector.tensor_scalar(
                out=pages[i][:], in0=h_tiles[i][:], scalar1=column("low", i), scalar2=None, op0=ALU.max
            )

        def put(i):
            nc.vector.tensor_tensor(
                out=pages[i][:].indirect(pos2_t[:]), in0=looks[i][:], in1=signed[:, i, :], op=ALU.mult
            )

        def round_page(engine, i, cols):
            b, t = divmod(i, PACK)
            if engine == "vector":
                nc.vector.tensor_scalar(
                    out=rounded[b][:, t, cols], in0=pages[i][:, cols], scalar1=column("gain", i),
                    scalar2=None, op0=ALU.mult,
                )
            else:
                nc.scalar.activation(
                    out=rounded[b][:, t, cols], in_=pages[i][:, cols], func=ACT.Copy, scale=column("gain", i)
                )

        def w1_late(a):
            grouped = kept("h%d" % a, [P, PACK * BANK], BF16)
            for c in range(2):
                group_w1("scalar", grouped, w1_raw[1, a][:, :, c * 256 : (c + 1) * 256], 64 * c, 64)
            w1_q[1, a] = quantise("w1_1%d" % a, grouped, 1)

        w3_q, page_q = {}, {}

        def w3_pass(b):
            grouped = kept("h%d" % (4 + b), [P, PACK * BANK], BF16)
            for c in range(2):
                group_plain("scalar", grouped, w3_raw[b][:, :, c * 256 : (c + 1) * 256], 256 * c, 256)
            w3_q[b] = quantise("w3_%d" % b, grouped, 1)

        def group_page_half(half):
            grouped = grouped_tile()
            for c in range(2):
                first = half * BANK + c * 256
                group_plain("scalar", grouped, rounded[0][:, :, first : first + 256], 256 * c, 256)
            return grouped

        def readout_pass(acc, which, n, b, half, cols, start, stop):
            codes, scales = page_q[b, half]
            if which == 2:
                weight = w2_codes[:, b, 2 * P * n : 2 * P * (n + 1)].bitcast(FP4X4)
                weight_scale = w2_planes[:, b, P * n : P * (n + 1)]
            else:
                weight = w3_q[b][0][:, P * n : P * (n + 1)].bitcast(FP8X4)
                weight_scale = w3_q[b][1][:, P * n : P * (n + 1)]
            nc.tensor.matmul_mx(
                out=acc[:, cols], lhsT=weight, lhsT_scale=weight_scale,
                rhs=codes[:, cols].bitcast(FP8X4), rhs_scale=scales[:, cols], start=start, stop=stop,
            )

        def readout_bank(which, n):
            return bank(4 + n if which == 2 else n)

        whole = slice(0, BANK)
        y_acc = {}
        for a in range(K_PASSES - 1):
            for i in range(2):
                first_pass(i, a)
        early_groups = []
        for step in range(ROW_TILES + 1):
            if step < ROW_TILES:
                for a in range(K_PASSES - 1 if step < 2 else 0, K_PASSES):
                    first_pass(step, a)
                add_base(step)
                look(step)
            if step == ROW_TILES:
                page_q[0, 0] = quantise("page_00", early_groups[0], 1, "h7")
                for which in (2, 3):
                    for n in range(N_TILES):
                        y_acc[which, n] = readout_bank(which, n)
                        readout_pass(y_acc[which, n], which, n, 0, 0, whole, True, False)
            if step >= 1:
                put(step - 1)
            if step < ROW_TILES:
                floor(step)
            if 1 <= step < ROW_TILES:
                round_page("scalar", step - 1, slice(0, S))
            if step < K_PASSES:
                w1_late(step)
            if step in (4, 7):
                early_groups.append(group_page_half((step - 4) // 3))
            if step in (5, 6):
                w3_pass(step - 5)
        page_q[0, 1] = quantise("page_01", early_groups[1], 1)

        last = ROW_TILES - 1
        QUARTER = 256
        round_page("vector", last, slice(0, QUARTER))
        round_page("scalar", last, slice(QUARTER, BANK))
        round_page("scalar", last, slice(BANK, S))
        for half in range(HALVES):
            page_q[1, half] = (kept("page_1%d_codes" % half, [P, BANK], U32), kept("page_1%d_scales" % half, [P, BANK], U8))
        for q in range(4):
            grouped = ring.tile([P, PACK * QUARTER], BF16, name="grouped_half", tag="grouped_half", bufs=3, align_bytes=64)
            group_plain("scalar" if q == 3 else "vector", grouped, rounded[1][:, :, q * QUARTER : (q + 1) * QUARTER], 0, QUARTER)
            half, part = divmod(q, 2)
            cols = slice(part * QUARTER, (part + 1) * QUARTER)
            codes, scales = page_q[1, half]
            nc.vector.quantize_mx(out=codes[:, cols].bitcast(FP8X4), scales=scales[:, cols], in_=grouped[:])
            if half == 0:
                for n in range(N_TILES):
                    for which in (2, 3):
                        readout_pass(y_acc[which, n], which, n, 1, 0, cols, False, part == 1)

        def finish(n, half, acc2, acc3):
            result = kept("result%d%d" % (n, half), [P, BANK], F32)
            nc.scalar.copy(out=result[:], in_=acc2[:])
            nc.vector.tensor_tensor(out=result[:], in0=acc3[:], in1=result[:], op=ALU.max)
            nc.sync.dma_start(out=out[P * n : P * (n + 1), half * BANK : (half + 1) * BANK], in_=result[:])

        for n in range(N_TILES):
            finish(n, 0, y_acc[2, n], y_acc[3, n])
        for n in range(N_TILES):
            accs = []
            for which in (2, 3):
                acc = readout_bank(which, n)
                for b in range(R_PASSES):
                    readout_pass(acc, which, n, b, 1, whole, b == 0, b == R_PASSES - 1)
                accs.append(acc)
            finish(n, 1, accs[0], accs[1])
